import numpy as np
import ml_dtypes


def mxq(x, axis, fmt="e4m3"):
    dtype, down = {"e4m3": (ml_dtypes.float8_e4m3fn, 7), "e5m2": (ml_dtypes.float8_e5m2, 14)}[fmt]
    v = np.moveaxis(np.asarray(x, np.float32).astype(ml_dtypes.bfloat16).astype(np.float64), axis, -1)
    blocks = v.reshape(v.shape[:-1] + (-1, 32))
    amax = np.abs(blocks).max(-1, keepdims=True)
    byte = np.maximum(np.where(amax > 0, np.frexp(amax)[1] - 1 + 127, 0) - down, 1)
    scale = np.exp2(byte - 127.0)
    codes = (blocks / scale).astype(np.float32).astype(dtype).astype(np.float64)
    return np.moveaxis((codes * scale).reshape(v.shape), -1, axis)


WIDE = False


def mx_kscale(k):
    if not WIDE:
        return np.ones(k)
    levels = np.array([10, -10, 5, -5, 0])
    if k % 512:
        return np.exp2(np.random.permutation(np.resize(levels, k // 32))).repeat(32)
    a = np.empty((k // 512, 16))
    for p in range(k // 512):
        a[p, :8] = np.random.permutation(np.resize(levels, 8))
        for g in range(8):
            far = levels[np.abs(levels - a[p, g]) >= 10]
            a[p, g + 8] = far[np.random.randint(len(far))]
    return np.exp2(a.ravel()).repeat(32)


def f64(x):
    return np.asarray(x).astype(np.float64)


def striped(idx):
    return np.tile(idx.reshape(-1, 16).T, (8, 1)).astype(np.uint16)


def unstriped(offs):
    return offs[:16].T.reshape(-1).astype(np.int64)


def relu2(v):
    return np.maximum(v, 0.0) ** 2


K, T, E, C, N = 2560, 512, 4, 256, 384


def by_expert(wq, xq):
    return np.concatenate([wq[e].T @ xq[:, e * C:(e + 1) * C] for e in range(E)], axis=1)


def setup_inputs():
    n = np.random.standard_normal
    s = mx_kscale(K)[:, None]
    first = np.random.permutation(np.repeat(np.arange(E), T // E))
    second = (first + 1 + np.random.permutation(np.repeat(np.arange(E - 1), -(-T // (E - 1)))[:T])) % E
    while np.bincount(second, minlength=E).max() != T // E:
        load = np.bincount(second, minlength=E); hi, lo = int(load.argmax()), int(load.argmin())
        t = np.flatnonzero((second == hi) & (first != lo))[0]; second[t] = lo
    slot_token = np.empty(E * C, np.int64); pos = np.empty((2, T), np.int64); fill = np.zeros(E, np.int64)
    place = np.stack([np.random.permutation(C) for _ in range(E)])
    for r, deal in enumerate((first, second)):
        for t in np.random.permutation(T):
            e = deal[t]; j = e * C + place[e, fill[e]]; fill[e] += 1; slot_token[j] = t; pos[r, t] = j
    g = np.random.uniform(0.2, 0.8, T)
    return {
        "xT": (n((K, T)) * s).astype(np.float32),
        "w": (n((E, K, N)) / np.sqrt(K) / s[None]).astype(np.float32),
        "b": (0.3 * n((N, E))).astype(np.float32),
        "gate": np.stack([np.tile(g, (N, 1)), np.tile(1.0 - g, (N, 1))]).astype(np.float32),
        "offs": striped(slot_token),
        "pos1": striped(pos[0]),
        "pos2": striped(pos[1]),
    }


def reference(xT, w, b, gate, offs, pos1, pos2):
    idx = unstriped(offs)
    xq = mxq(f64(xT)[:, idx], 0, "e4m3")
    y = by_expert(mxq(f64(w), 1, "e4m3"), xq)
    y = relu2(y + np.repeat(f64(b), C, axis=1))
    return f64(gate[0]) * y[:, unstriped(pos1)] + f64(gate[1]) * y[:, unstriped(pos2)]

@@ -1,0 +1,195 @@
+from contextlib import ExitStack
+
+import concourse.mybir as mybir
+
+K, T, E, C, N = 2560, 512, 4, 256, 384
+
+F32 = mybir.dt.float32
+BF16 = mybir.dt.bfloat16
+U32 = mybir.dt.uint32
+U16 = mybir.dt.uint16
+U8 = mybir.dt.uint8
+FP8X4 = mybir.dt.float8_e4m3fn_x4
+RELU = mybir.ActivationFunctionType.Relu
+SQUARE = mybir.ActivationFunctionType.Square
+MULT = mybir.AluOpType.mult
+ADD = mybir.AluOpType.add
+
+P = 128
+PACK = 4
+K_PASS = P * PACK
+PASSES = K // K_PASS
+BLOCKS = N // P
+SLOTS = E * C
+CUTS = ((0, 384), (384, 768), (768, 1024))
+TAIL = (3, 4)
+
+FLOPS = 2 * K * N * E * C
+
+X_VECTOR = (0, 2, 4)
+W_VECTOR = (8, 10, 12, 14, 16, 17)
+
+
+def interleave(nc, on_vector, grouped, raw):
+    dst = grouped.rearrange("p (c i t) -> p c t i", i=4, t=PACK)
+    src = raw.rearrange("p t (c i) -> p c t i", i=4)
+    if on_vector:
+        nc.vector.tensor_copy(out=dst, in_=src)
+    else:
+        nc.scalar.copy(out=dst, in_=src)
+
+
+def tile_routed_moe_kernel(tc, xT, w, b, gate, offs, pos1, pos2, out):
+    nc = tc.nc
+    with ExitStack() as ctx:
+        keep = ctx.enter_context(tc.tile_pool(name="keep", bufs=1))
+        stage = ctx.enter_context(tc.tile_pool(name="stage", bufs=2))
+        psum = ctx.enter_context(tc.psum_pool(name="psum", bufs=8))
+
+        offs_sb = keep.tile([P, SLOTS // 16], U16, name="offs_sb")
+        pos1_sb = keep.tile([P, T // 16], U16, name="pos1_sb")
+        pos2_sb = keep.tile([P, T // 16], U16, name="pos2_sb")
+        bias = keep.tile([P, BLOCKS, E], F32, name="bias")
+
+        planes4 = keep.tile([P, T], U8, name="planes4", align_bytes=64)
+        plane1 = keep.tile([P, T], U8, name="plane1", align_bytes=64)
+        slot_planes4 = keep.tile([P, SLOTS], U8, name="slot_planes4", align_bytes=64)
+        slot_plane1 = keep.tile([P, SLOTS], U8, name="slot_plane1", align_bytes=64)
+        nc.gpsimd.memset(planes4[:], 0)
+        nc.gpsimd.memset(plane1[:], 0)
+
+        x_rows = xT.rearrange("(g p j) t -> g p j t", p=P, j=PACK)
+        w_rows = w.rearrange("e (g p j) n -> e g p j n", p=P, j=PACK)
+
+        x_raw = []
+        for a in range(PASSES):
+            raw = stage.tile([P, PACK, T], F32, name="raw", tag="raw", bufs=11)
+            nc.sync.dma_start(out=raw[:], in_=x_rows[a])
+            x_raw.append(raw)
+            if a == 0:
+                nc.sync.dma_start(out=offs_sb[:], in_=offs)
+            if a == 2:
+                nc.sync.dma_start(out=bias[:], in_=b.rearrange("(c p) e -> p c e", p=P))
+
+        x_codes = []
+        for a in range(PASSES):
+            grouped = stage.tile([P, T * PACK], BF16, name="x_grouped", tag="x_grouped", bufs=3, align_bytes=64)
+            interleave(nc, a in X_VECTOR, grouped[:], x_raw[a][:])
+            codes = keep.tile([P, T], U32, name=f"x_codes{a}", align_bytes=64)
+            scales = planes4[4 * a : P, :] if a < 4 else plane1[:]
+            nc.vector.quantize_mx(out=codes[:].bitcast(FP8X4), scales=scales, in_=grouped[:])
+            x_codes.append(codes)
+
+        slot_codes = []
+        gathers = []
+        for a in range(PASSES):
+            codes = keep.tile([P, SLOTS], U32, name=f"slot_codes{a}", align_bytes=64)
+            slot_codes.append(codes)
+            for lo, hi in CUTS:
+                gathers.append((codes, x_codes[a], lo, hi))
+            if a == 3:
+                for lo, hi in CUTS:
+                    gathers.append((slot_planes4, planes4, lo, hi))
+            if a == 4:
+                for lo, hi in CUTS:
+                    gathers.append((slot_plane1, plane1, lo, hi))
+
+        def gather(count):
+            for g in range(min(count, len(gathers))):
+                dst, src, lo, hi = gathers[0]
+                gathers.remove(gathers[0])
+                nc.vector.tensor_copy(out=dst[:, lo:hi], in_=src[:].indirect(offs_sb[:, lo // 16 : hi // 16]))
+
+        def multiply(acc, e, a, w_codes, w_scales):
+            cols = slice(e * C, (e + 1) * C)
+            planes = slot_planes4[4 * a : P, cols] if a < 4 else slot_plane1[:, cols]
+            nc.tensor.matmul_mx(
+                out=acc[:],
+                lhsT=w_codes.bitcast(FP8X4),
+                lhsT_scale=w_scales,
+                rhs=slot_codes[a][:, cols].bitcast(FP8X4),
+                rhs_scale=planes,
+                start=(a == 0),
+                stop=(a == PASSES - 1),
+            )
+
+        y = []
+        for n in range(BLOCKS):
+            y_block = keep.tile([P, SLOTS], F32, name=f"y{n}")
+            y.append(y_block)
+
+        def activate(acc, e, n):
+            r = stage.tile([P, C], F32, name="r", tag="r", bufs=4)
+            nc.scalar.activation(out=r[:], in_=acc[:], func=RELU, bias=bias[:, n, e : e + 1])
+            nc.scalar.activation(out=y[n][:, e * C : (e + 1) * C], in_=r[:], func=SQUARE)
+
+        unit = 0
+        pending = []
+        acc = {}
+        for e in range(E):
+            for n in range(BLOCKS):
+                acc_tile = psum.tile([P, C], F32, name="acc", tag="acc")
+                acc[(e, n)] = acc_tile
+            for a in range(PASSES):
+                if e == E - 1 and a in TAIL:
+                    continue
+                raw = stage.tile([P, PACK, N], F32, name="w_raw", tag="raw", bufs=11)
+                nc.sync.dma_start(out=raw[:], in_=w_rows[e, a])
+                grouped = stage.tile([P, N * PACK], BF16, name="w_grouped", tag="w_grouped", bufs=5, align_bytes=64)
+                interleave(nc, unit in W_VECTOR, grouped[:], raw[:])
+                codes = stage.tile([P, N], U32, name="w_codes", tag="w_codes", bufs=8, align_bytes=64)
+                scales = stage.tile([P, N], U8, name="w_scales", tag="w_scales", bufs=8, align_bytes=64)
+                for lo, hi in ((0, 256), (256, 384)):
+                    nc.vector.quantize_mx(
+                        out=codes[:, lo:hi].bitcast(FP8X4),
+                        scales=scales[:, lo:hi],
+                        in_=grouped[:, PACK * lo : PACK * hi],
+                    )
+                gather(4)
+                pending.append((e, a, codes, scales))
+                if len(gathers) == 0:
+                    for pe, pa, pcodes, pscales in pending:
+                        for n in range(BLOCKS):
+                            cols = slice(n * P, (n + 1) * P)
+                            multiply(acc[(pe, n)], pe, pa, pcodes[:, cols], pscales[:, cols])
+                        if pa == PASSES - 1:
+                            for n in range(BLOCKS):
+                                activate(acc[(pe, n)], pe, n)
+                    pending.clear()
+                if unit == 1:
+                    nc.sync.dma_start(out=pos1_sb[:], in_=pos1)
+                    nc.sync.dma_start(out=pos2_sb[:], in_=pos2)
+                unit += 1
+
+        gates = []
+
+        def finish_sums(n):
+            for a in TAIL:
+                raw = stage.tile([P, PACK, P], F32, name="t_raw", tag="t_raw", bufs=6)
+                nc.sync.dma_start(out=raw[:], in_=w_rows[E - 1, a, :, :, n * P : (n + 1) * P])
+                grouped = stage.tile([P, P * PACK], BF16, name="t_grouped", tag="t_grouped", bufs=4, align_bytes=64)
+                interleave(nc, n == 0, grouped[:], raw[:])
+                codes = stage.tile([P, P], U32, name="t_codes", tag="t_codes", bufs=6, align_bytes=64)
+                scales = stage.tile([P, P], U8, name="t_scales", tag="t_scales", bufs=6, align_bytes=64)
+                nc.vector.quantize_mx(out=codes[:].bitcast(FP8X4), scales=scales[:], in_=grouped[:])
+                multiply(acc[(E - 1, n)], E - 1, a, codes[:], scales[:])
+            activate(acc[(E - 1, n)], E - 1, n)
+            gate_sb = keep.tile([P, 2, T], F32, name=f"gate{n}")
+            nc.sync.dma_start(out=gate_sb[:], in_=gate[:, n * P : (n + 1) * P, :].rearrange("r p t -> p r t"))
+            gates.append(gate_sb)
+
+        def combine(n):
+            first = stage.tile([P, T], F32, name="first", tag="first", bufs=2)
+            second = stage.tile([P, T], F32, name="second", tag="second", bufs=2)
+            nc.vector.tensor_tensor(out=first[:], in0=y[n][:].indirect(pos1_sb[:]), in1=gates[n][:, 0, :], op=MULT)
+            nc.vector.tensor_tensor(out=second[:], in0=y[n][:].indirect(pos2_sb[:]), in1=gates[n][:, 1, :], op=MULT)
+            result = stage.tile([P, T], F32, name="result", tag="result", bufs=3)
+            nc.vector.tensor_tensor(out=result[:], in0=first[:], in1=second[:], op=ADD)
+            nc.sync.dma_start(out=out[n * P : (n + 1) * P, :], in_=result[:])
+
+        finish_sums(0)
+        finish_sums(1)
+        combine(0)
+        finish_sums(2)
+        combine(1)
+        combine(2)

@@ -26,17 +26,24 @@ TAIL = (3, 4)
 
 FLOPS = 2 * K * N * E * C
 
-X_VECTOR = (0, 2, 4)
-W_VECTOR = (8, 10, 12, 14, 16, 17)
+RAW = 13
+X_ENGINES = "VSSSS"
+W_ENGINES = "SSSSSSSSVVSVVVSVSV"
+T_ENGINES = ("VV", "VV", "SS")
 
 
-def interleave(nc, on_vector, grouped, raw):
+def interleave(nc, engine, grouped, raw):
     dst = grouped.rearrange("p (c i t) -> p c t i", i=4, t=PACK)
     src = raw.rearrange("p t (c i) -> p c t i", i=4)
-    if on_vector:
+    if engine == "V":
         nc.vector.tensor_copy(out=dst, in_=src)
-    else:
+    elif engine == "S":
         nc.scalar.copy(out=dst, in_=src)
+    else:
+        half = dst.shape[1] // 2
+        for lo in (0, half):
+            part = slice(lo, lo + half)
+            nc.gpsimd.tensor_scalar(out=dst[:, part], in0=src[:, part], scalar1=1.0, scalar2=0.0, op0=MULT, op1=ADD)
 
 
 def tile_routed_moe_kernel(tc, xT, w, b, gate, offs, pos1, pos2, out):
@@ -63,8 +70,9 @@ def tile_routed_moe_kernel(tc, xT, w, b, gate, offs, pos1, pos2, out):
 
         x_raw = []
         for a in range(PASSES):
-            raw = stage.tile([P, PACK, T], F32, name="raw", tag="raw", bufs=11)
-            nc.sync.dma_start(out=raw[:], in_=x_rows[a])
+            raw = stage.tile([P, PACK, T], F32, name="raw", tag="raw", bufs=RAW)
+            for lo, hi in ((0, 256), (256, 512)) if a == 0 else ((0, 512),):
+                nc.sync.dma_start(out=raw[:, :, lo:hi], in_=x_rows[a, :, :, lo:hi])
             x_raw.append(raw)
             if a == 0:
                 nc.sync.dma_start(out=offs_sb[:], in_=offs)
@@ -74,7 +82,8 @@ def tile_routed_moe_kernel(tc, xT, w, b, gate, offs, pos1, pos2, out):
         x_codes = []
         for a in range(PASSES):
             grouped = stage.tile([P, T * PACK], BF16, name="x_grouped", tag="x_grouped", bufs=3, align_bytes=64)
-            interleave(nc, a in X_VECTOR, grouped[:], x_raw[a][:])
+            for lo, hi in ((0, 256), (256, 512)) if a == 0 else ((0, 512),):
+                interleave(nc, X_ENGINES[a], grouped[:, PACK * lo : PACK * hi], x_raw[a][:, :, lo:hi])
             codes = keep.tile([P, T], U32, name=f"x_codes{a}", align_bytes=64)
             scales = planes4[4 * a : P, :] if a < 4 else plane1[:]
             nc.vector.quantize_mx(out=codes[:].bitcast(FP8X4), scales=scales, in_=grouped[:])
@@ -119,9 +128,10 @@ def tile_routed_moe_kernel(tc, xT, w, b, gate, offs, pos1, pos2, out):
             y.append(y_block)
 
         def activate(acc, e, n):
-            r = stage.tile([P, C], F32, name="r", tag="r", bufs=4)
-            nc.scalar.activation(out=r[:], in_=acc[:], func=RELU, bias=bias[:, n, e : e + 1])
-            nc.scalar.activation(out=y[n][:, e * C : (e + 1) * C], in_=r[:], func=SQUARE)
+            nc.scalar.activation(out=y[n][:, e * C : (e + 1) * C], in_=acc[:], func=RELU, bias=bias[:, n, e : e + 1])
+            if e >= 1:
+                done = y[n][:, 0 : 2 * C] if e == 1 else y[n][:, e * C : (e + 1) * C]
+                nc.scalar.activation(out=done, in_=done, func=SQUARE)
 
         unit = 0
         pending = []
@@ -133,21 +143,24 @@ def tile_routed_moe_kernel(tc, xT, w, b, gate, offs, pos1, pos2, out):
             for a in range(PASSES):
                 if e == E - 1 and a in TAIL:
                     continue
-                raw = stage.tile([P, PACK, N], F32, name="w_raw", tag="raw", bufs=11)
+                raw = stage.tile([P, PACK, N], F32, name="w_raw", tag="raw", bufs=RAW)
                 nc.sync.dma_start(out=raw[:], in_=w_rows[e, a])
-                grouped = stage.tile([P, N * PACK], BF16, name="w_grouped", tag="w_grouped", bufs=5, align_bytes=64)
-                interleave(nc, unit in W_VECTOR, grouped[:], raw[:])
-                codes = stage.tile([P, N], U32, name="w_codes", tag="w_codes", bufs=8, align_bytes=64)
-                scales = stage.tile([P, N], U8, name="w_scales", tag="w_scales", bufs=8, align_bytes=64)
-                for lo, hi in ((0, 256), (256, 384)):
-                    nc.vector.quantize_mx(
-                        out=codes[:, lo:hi].bitcast(FP8X4),
-                        scales=scales[:, lo:hi],
-                        in_=grouped[:, PACK * lo : PACK * hi],
-                    )
-                gather(4)
-                pending.append((e, a, codes, scales))
-                if len(gathers) == 0:
+                half = unit % 2
+                if half == 0:
+                    grouped = stage.tile([P, 2 * N * PACK], BF16, name="w_grouped", tag="w_grouped", bufs=3, align_bytes=64)
+                    codes = stage.tile([P, 2 * N], U32, name="w_codes", tag="w_codes", bufs=5, align_bytes=64)
+                    scales = stage.tile([P, 2 * N], U8, name="w_scales", tag="w_scales", bufs=5, align_bytes=64)
+                interleave(nc, W_ENGINES[unit], grouped[:, half * N * PACK : (half + 1) * N * PACK], raw[:])
+                if half == 1:
+                    for lo, hi in ((0, 512), (512, 768)):
+                        nc.vector.quantize_mx(
+                            out=codes[:, lo:hi].bitcast(FP8X4),
+                            scales=scales[:, lo:hi],
+                            in_=grouped[:, PACK * lo : PACK * hi],
+                        )
+                gather(3)
+                pending.append((e, a, codes[:, half * N : (half + 1) * N], scales[:, half * N : (half + 1) * N]))
+                if len(gathers) == 0 and half == 1:
                     for pe, pa, pcodes, pscales in pending:
                         for n in range(BLOCKS):
                             cols = slice(n * P, (n + 1) * P)
@@ -164,19 +177,25 @@ def tile_routed_moe_kernel(tc, xT, w, b, gate, offs, pos1, pos2, out):
         gates = []
 
         def finish_sums(n):
-            for a in TAIL:
-                raw = stage.tile([P, PACK, P], F32, name="t_raw", tag="t_raw", bufs=6)
-                nc.sync.dma_start(out=raw[:], in_=w_rows[E - 1, a, :, :, n * P : (n + 1) * P])
-                grouped = stage.tile([P, P * PACK], BF16, name="t_grouped", tag="t_grouped", bufs=4, align_bytes=64)
-                interleave(nc, n == 0, grouped[:], raw[:])
-                codes = stage.tile([P, P], U32, name="t_codes", tag="t_codes", bufs=6, align_bytes=64)
-                scales = stage.tile([P, P], U8, name="t_scales", tag="t_scales", bufs=6, align_bytes=64)
-                nc.vector.quantize_mx(out=codes[:].bitcast(FP8X4), scales=scales[:], in_=grouped[:])
-                multiply(acc[(E - 1, n)], E - 1, a, codes[:], scales[:])
-            activate(acc[(E - 1, n)], E - 1, n)
-            gate_sb = keep.tile([P, 2, T], F32, name=f"gate{n}")
-            nc.sync.dma_start(out=gate_sb[:], in_=gate[:, n * P : (n + 1) * P, :].rearrange("r p t -> p r t"))
+            cols = slice(n * P, (n + 1) * P)
+            raw = stage.tile([P, len(TAIL), PACK, P], F32, name="t_raw", tag="raw", bufs=RAW)
+            for i, a in enumerate(TAIL):
+                nc.sync.dma_start(out=raw[:, i], in_=w_rows[E - 1, a, :, :, cols])
+            gate_sb = stage.tile([P, 2, T], F32, name="gate_sb", tag="raw", bufs=RAW)
+            nc.sync.dma_start(out=gate_sb[:], in_=gate[:, cols, :].rearrange("r p t -> p r t"))
             gates.append(gate_sb)
+            grouped = stage.tile([P, len(TAIL), P * PACK], BF16, name="t_grouped", tag="t_grouped", bufs=3, align_bytes=64)
+            codes = stage.tile([P, len(TAIL) * P], U32, name="t_codes", tag="t_codes", bufs=3, align_bytes=64)
+            scales = stage.tile([P, len(TAIL) * P], U8, name="t_scales", tag="t_scales", bufs=3, align_bytes=64)
+            for i, a in enumerate(TAIL):
+                interleave(nc, T_ENGINES[n][i], grouped[:, i], raw[:, i])
+            nc.vector.quantize_mx(
+                out=codes[:].bitcast(FP8X4), scales=scales[:], in_=grouped[:].rearrange("p i f -> p (i f)")
+            )
+            for i, a in enumerate(TAIL):
+                part = slice(i * P, (i + 1) * P)
+                multiply(acc[(E - 1, n)], E - 1, a, codes[:, part], scales[:, part])
+            activate(acc[(E - 1, n)], E - 1, n)
 
         def combine(n):
             first = stage.tile([P, T], F32, name="first", tag="first", bufs=2)

@@ -22,14 +22,13 @@ PASSES = K // K_PASS
 BLOCKS = N // P
 SLOTS = E * C
 CUTS = ((0, 384), (384, 768), (768, 1024))
-TAIL = (3, 4)
 
 FLOPS = 2 * K * N * E * C
 
 RAW = 13
 X_ENGINES = "VSSSS"
-W_ENGINES = "SSSSSSSSVVSVVVSVSV"
-T_ENGINES = ("VV", "VV", "SS")
+W_ENGINES = "SGSSSGSSSGVVVVV"
+GATHERS = 6
 
 
 def interleave(nc, engine, grouped, raw):
@@ -40,9 +39,9 @@ def interleave(nc, engine, grouped, raw):
     elif engine == "S":
         nc.scalar.copy(out=dst, in_=src)
     else:
-        half = dst.shape[1] // 2
-        for lo in (0, half):
-            part = slice(lo, lo + half)
+        quarter = dst.shape[1] // 4
+        for lo in (0, quarter, 2 * quarter, 3 * quarter):
+            part = slice(lo, lo + quarter)
             nc.gpsimd.tensor_scalar(out=dst[:, part], in0=src[:, part], scalar1=1.0, scalar2=0.0, op0=MULT, op1=ADD)
 
 
@@ -109,11 +108,11 @@ def tile_routed_moe_kernel(tc, xT, w, b, gate, offs, pos1, pos2, out):
                 gathers.remove(gathers[0])
                 nc.vector.tensor_copy(out=dst[:, lo:hi], in_=src[:].indirect(offs_sb[:, lo // 16 : hi // 16]))
 
-        def multiply(acc, e, a, w_codes, w_scales):
+        def multiply(acc_tile, e, a, w_codes, w_scales):
             cols = slice(e * C, (e + 1) * C)
             planes = slot_planes4[4 * a : P, cols] if a < 4 else slot_plane1[:, cols]
             nc.tensor.matmul_mx(
-                out=acc[:],
+                out=acc_tile[:],
                 lhsT=w_codes.bitcast(FP8X4),
                 lhsT_scale=w_scales,
                 rhs=slot_codes[a][:, cols].bitcast(FP8X4),
@@ -127,8 +126,8 @@ def tile_routed_moe_kernel(tc, xT, w, b, gate, offs, pos1, pos2, out):
             y_block = keep.tile([P, SLOTS], F32, name=f"y{n}")
             y.append(y_block)
 
-        def activate(acc, e, n):
-            nc.scalar.activation(out=y[n][:, e * C : (e + 1) * C], in_=acc[:], func=RELU, bias=bias[:, n, e : e + 1])
+        def activate(acc_tile, e, n):
+            nc.scalar.activation(out=y[n][:, e * C : (e + 1) * C], in_=acc_tile[:], func=RELU, bias=bias[:, n, e : e + 1])
             if e >= 1:
                 done = y[n][:, 0 : 2 * C] if e == 1 else y[n][:, e * C : (e + 1) * C]
                 nc.scalar.activation(out=done, in_=done, func=SQUARE)
@@ -136,13 +135,11 @@ def tile_routed_moe_kernel(tc, xT, w, b, gate, offs, pos1, pos2, out):
         unit = 0
         pending = []
         acc = {}
-        for e in range(E):
+        for e in range(E - 1):
             for n in range(BLOCKS):
                 acc_tile = psum.tile([P, C], F32, name="acc", tag="acc")
                 acc[(e, n)] = acc_tile
             for a in range(PASSES):
-                if e == E - 1 and a in TAIL:
-                    continue
                 raw = stage.tile([P, PACK, N], F32, name="w_raw", tag="raw", bufs=RAW)
                 nc.sync.dma_start(out=raw[:], in_=w_rows[e, a])
                 half = unit % 2
@@ -151,16 +148,17 @@ def tile_routed_moe_kernel(tc, xT, w, b, gate, offs, pos1, pos2, out):
                     codes = stage.tile([P, 2 * N], U32, name="w_codes", tag="w_codes", bufs=5, align_bytes=64)
                     scales = stage.tile([P, 2 * N], U8, name="w_scales", tag="w_scales", bufs=5, align_bytes=64)
                 interleave(nc, W_ENGINES[unit], grouped[:, half * N * PACK : (half + 1) * N * PACK], raw[:])
-                if half == 1:
-                    for lo, hi in ((0, 512), (512, 768)):
+                last = unit == (E - 1) * PASSES - 1
+                if half == 1 or last:
+                    for lo, hi in ((0, 512), (512, 768)) if half == 1 else ((0, 256), (256, 384)):
                         nc.vector.quantize_mx(
                             out=codes[:, lo:hi].bitcast(FP8X4),
                             scales=scales[:, lo:hi],
                             in_=grouped[:, PACK * lo : PACK * hi],
                         )
-                gather(3)
+                gather(GATHERS)
                 pending.append((e, a, codes[:, half * N : (half + 1) * N], scales[:, half * N : (half + 1) * N]))
-                if len(gathers) == 0 and half == 1:
+                if len(gathers) == 0 and (half == 1 or last):
                     for pe, pa, pcodes, pscales in pending:
                         for n in range(BLOCKS):
                             cols = slice(n * P, (n + 1) * P)
@@ -174,28 +172,44 @@ def tile_routed_moe_kernel(tc, xT, w, b, gate, offs, pos1, pos2, out):
                     nc.sync.dma_start(out=pos2_sb[:], in_=pos2)
                 unit += 1
 
-        gates = []
+        e = E - 1
+        gates = {}
+        for n in range(BLOCKS):
+            acc_tile = psum.tile([P, C], F32, name="acc", tag="acc")
+            acc[(e, n)] = acc_tile
 
-        def finish_sums(n):
-            cols = slice(n * P, (n + 1) * P)
-            raw = stage.tile([P, len(TAIL), PACK, P], F32, name="t_raw", tag="raw", bufs=RAW)
-            for i, a in enumerate(TAIL):
-                nc.sync.dma_start(out=raw[:, i], in_=w_rows[E - 1, a, :, :, cols])
+        def load_gate(n):
             gate_sb = stage.tile([P, 2, T], F32, name="gate_sb", tag="raw", bufs=RAW)
-            nc.sync.dma_start(out=gate_sb[:], in_=gate[:, cols, :].rearrange("r p t -> p r t"))
-            gates.append(gate_sb)
-            grouped = stage.tile([P, len(TAIL), P * PACK], BF16, name="t_grouped", tag="t_grouped", bufs=3, align_bytes=64)
-            codes = stage.tile([P, len(TAIL) * P], U32, name="t_codes", tag="t_codes", bufs=3, align_bytes=64)
-            scales = stage.tile([P, len(TAIL) * P], U8, name="t_scales", tag="t_scales", bufs=3, align_bytes=64)
-            for i, a in enumerate(TAIL):
-                interleave(nc, T_ENGINES[n][i], grouped[:, i], raw[:, i])
-            nc.vector.quantize_mx(
-                out=codes[:].bitcast(FP8X4), scales=scales[:], in_=grouped[:].rearrange("p i f -> p (i f)")
-            )
-            for i, a in enumerate(TAIL):
-                part = slice(i * P, (i + 1) * P)
-                multiply(acc[(E - 1, n)], E - 1, a, codes[:, part], scales[:, part])
-            activate(acc[(E - 1, n)], E - 1, n)
+            nc.sync.dma_start(out=gate_sb[:], in_=gate[:, n * P : (n + 1) * P, :].rearrange("r p t -> p r t"))
+            gates[n] = gate_sb
+
+        def chunk(blocks, passes, engines):
+            width = len(blocks) * P
+            cols = slice(blocks[0] * P, blocks[0] * P + width)
+            raw = stage.tile([P, len(passes), PACK, width], F32, name="t_raw", tag="raw", bufs=RAW)
+            grouped = stage.tile([P, len(passes) * width * PACK], BF16, name="t_grouped", tag="t_grouped", bufs=3, align_bytes=64)
+            codes = stage.tile([P, len(passes) * width], U32, name="t_codes", tag="t_codes", bufs=4, align_bytes=64)
+            scales = stage.tile([P, len(passes) * width], U8, name="t_scales", tag="t_scales", bufs=4, align_bytes=64)
+            for i, a in enumerate(passes):
+                nc.sync.dma_start(out=raw[:, i], in_=w_rows[e, a, :, :, cols])
+            for i in range(len(passes)):
+                interleave(nc, engines[i], grouped[:, i * width * PACK : (i + 1) * width * PACK], raw[:, i])
+            lo = 0
+            total = len(passes) * width
+            for words in (512, 256, 128):
+                if total - lo >= words:
+                    nc.vector.quantize_mx(
+                        out=codes[:, lo : lo + words].bitcast(FP8X4),
+                        scales=scales[:, lo : lo + words],
+                        in_=grouped[:, PACK * lo : PACK * (lo + words)],
+                    )
+                    lo += words
+            for i, a in enumerate(passes):
+                for n in blocks:
+                    part = slice(i * width + (n - blocks[0]) * P, i * width + (n - blocks[0] + 1) * P)
+                    multiply(acc[(e, n)], e, a, codes[:, part], scales[:, part])
+                    if a == PASSES - 1:
+                        activate(acc[(e, n)], e, n)
 
         def combine(n):
             first = stage.tile([P, T], F32, name="first", tag="first", bufs=2)
@@ -206,9 +220,17 @@ def tile_routed_moe_kernel(tc, xT, w, b, gate, offs, pos1, pos2, out):
             nc.vector.tensor_tensor(out=result[:], in0=first[:], in1=second[:], op=ADD)
             nc.sync.dma_start(out=out[n * P : (n + 1) * P, :], in_=result[:])
 
-        finish_sums(0)
-        finish_sums(1)
+        everything = (0, 1, 2)
+        chunk(everything, (0,), "V")
+        chunk(everything, (1,), "V")
+        chunk(everything, (2,), "V")
+        chunk(everything, (3,), "S")
+        chunk((0,), (4,), "S")
+        load_gate(0)
+        chunk((1,), (4,), "V")
+        load_gate(1)
         combine(0)
-        finish_sums(2)
+        chunk((2,), (4,), "S")
+        load_gate(2)
         combine(1)
         combine(2)

@@ -1,6 +1,7 @@
 from contextlib import ExitStack
 
 import concourse.mybir as mybir
+from concourse.masks import make_identity
 
 K, T, E, C, N = 2560, 512, 4, 256, 384
 
@@ -25,24 +26,40 @@ CUTS = ((0, 384), (384, 768), (768, 1024))
 
 FLOPS = 2 * K * N * E * C
 
-RAW = 13
-X_ENGINES = "VSSSS"
-W_ENGINES = "SGSSSGSSSGVVVVV"
-GATHERS = 6
+RAW = 12
+X_ENGINES = "SSBSH"
+W_ENGINES = ("S", "S", "S", "S", "S", "S", "S", "S", "S", "S", "H", "V", "V", "V", "V", "H", "V", "V", "W", "SBW")
+GROUP_SIZES = (2, 2, 2, 2, 2, 2, 2, 1, 2, 2, 1)
+GATHERS = 4
+SPLITS = {
+    "V": (("V", 1.0),),
+    "S": (("S", 1.0),),
+    "G": (("G", 1.0),),
+    "B": (("S", 2 / 3), ("V", 1 / 3)),
+    "H": (("S", 1 / 2), ("V", 1 / 2)),
+    "W": (("V", 2 / 3), ("S", 1 / 3)),
+    "J": (("S", 2 / 3), ("G", 1 / 3)),
+}
 
 
 def interleave(nc, engine, grouped, raw):
     dst = grouped.rearrange("p (c i t) -> p c t i", i=4, t=PACK)
     src = raw.rearrange("p t (c i) -> p c t i", i=4)
-    if engine == "V":
-        nc.vector.tensor_copy(out=dst, in_=src)
-    elif engine == "S":
-        nc.scalar.copy(out=dst, in_=src)
-    else:
-        quarter = dst.shape[1] // 4
-        for lo in (0, quarter, 2 * quarter, 3 * quarter):
-            part = slice(lo, lo + quarter)
-            nc.gpsimd.tensor_scalar(out=dst[:, part], in0=src[:, part], scalar1=1.0, scalar2=0.0, op0=MULT, op1=ADD)
+    groups = dst.shape[1]
+    lo = 0
+    for name, share in SPLITS[engine]:
+        hi = groups if name == SPLITS[engine][-1][0] else lo + int(groups * share + 0.5)
+        part = slice(lo, hi)
+        if name == "V":
+            nc.vector.tensor_copy(out=dst[:, part], in_=src[:, part])
+        elif name == "S":
+            nc.scalar.copy(out=dst[:, part], in_=src[:, part])
+        else:
+            for i in range(4):
+                step = (hi - lo) // 4
+                part = slice(lo + i * step, lo + (i + 1) * step)
+                nc.gpsimd.tensor_scalar(out=dst[:, part], in0=src[:, part], scalar1=1.0, scalar2=0.0, op0=MULT, op1=ADD)
+        lo = hi
 
 
 def tile_routed_moe_kernel(tc, xT, w, b, gate, offs, pos1, pos2, out):
@@ -63,6 +80,8 @@ def tile_routed_moe_kernel(tc, xT, w, b, gate, offs, pos1, pos2, out):
         slot_plane1 = keep.tile([P, SLOTS], U8, name="slot_plane1", align_bytes=64)
         nc.gpsimd.memset(planes4[:], 0)
         nc.gpsimd.memset(plane1[:], 0)
+        identity = keep.tile([P, P], F32, name="identity")
+        make_identity(nc, identity[:])
 
         x_rows = xT.rearrange("(g p j) t -> g p j t", p=P, j=PACK)
         w_rows = w.rearrange("e (g p j) n -> e g p j n", p=P, j=PACK)
@@ -80,7 +99,7 @@ def tile_routed_moe_kernel(tc, xT, w, b, gate, offs, pos1, pos2, out):
 
         x_codes = []
         for a in range(PASSES):
-            grouped = stage.tile([P, T * PACK], BF16, name="x_grouped", tag="x_grouped", bufs=3, align_bytes=64)
+            grouped = stage.tile([P, T * PACK], BF16, name="x_grouped", tag="grouped", bufs=6, align_bytes=64)
             for lo, hi in ((0, 256), (256, 512)) if a == 0 else ((0, 512),):
                 interleave(nc, X_ENGINES[a], grouped[:, PACK * lo : PACK * hi], x_raw[a][:, :, lo:hi])
             codes = keep.tile([P, T], U32, name=f"x_codes{a}", align_bytes=64)
@@ -112,7 +131,7 @@ def tile_routed_moe_kernel(tc, xT, w, b, gate, offs, pos1, pos2, out):
             cols = slice(e * C, (e + 1) * C)
             planes = slot_planes4[4 * a : P, cols] if a < 4 else slot_plane1[:, cols]
             nc.tensor.matmul_mx(
-                out=acc_tile[:],
+                out=acc_tile,
                 lhsT=w_codes.bitcast(FP8X4),
                 lhsT_scale=w_scales,
                 rhs=slot_codes[a][:, cols].bitcast(FP8X4),
@@ -127,110 +146,83 @@ def tile_routed_moe_kernel(tc, xT, w, b, gate, offs, pos1, pos2, out):
             y.append(y_block)
 
         def activate(acc_tile, e, n):
-            nc.scalar.activation(out=y[n][:, e * C : (e + 1) * C], in_=acc_tile[:], func=RELU, bias=bias[:, n, e : e + 1])
+            nc.scalar.activation(out=y[n][:, e * C : (e + 1) * C], in_=acc_tile, func=RELU, bias=bias[:, n, e : e + 1])
             if e >= 1:
                 done = y[n][:, 0 : 2 * C] if e == 1 else y[n][:, e * C : (e + 1) * C]
                 nc.scalar.activation(out=done, in_=done, func=SQUARE)
 
-        unit = 0
-        pending = []
         acc = {}
-        for e in range(E - 1):
-            for n in range(BLOCKS):
-                acc_tile = psum.tile([P, C], F32, name="acc", tag="acc")
-                acc[(e, n)] = acc_tile
-            for a in range(PASSES):
+        for n in range(BLOCKS):
+            pair = psum.tile([P, 2 * C], F32, name="acc_pair", tag="acc")
+            acc[(0, n)] = pair[:, 0:C]
+            acc[(1, n)] = pair[:, C : 2 * C]
+        units = [(e, a) for e in range(E) for a in range(PASSES)]
+        pending = []
+        first_unit = 0
+        for size in GROUP_SIZES:
+            grouped = stage.tile([P, size * N * PACK], BF16, name="w_grouped", tag="grouped", bufs=6, align_bytes=64)
+            codes = stage.tile([P, size * N], U32, name="w_codes", tag="w_codes", bufs=6, align_bytes=64)
+            scales = stage.tile([P, size * N], U8, name="w_scales", tag="w_scales", bufs=6, align_bytes=64)
+            for i in range(size):
+                e, a = units[first_unit + i]
                 raw = stage.tile([P, PACK, N], F32, name="w_raw", tag="raw", bufs=RAW)
                 nc.sync.dma_start(out=raw[:], in_=w_rows[e, a])
-                half = unit % 2
-                if half == 0:
-                    grouped = stage.tile([P, 2 * N * PACK], BF16, name="w_grouped", tag="w_grouped", bufs=3, align_bytes=64)
-                    codes = stage.tile([P, 2 * N], U32, name="w_codes", tag="w_codes", bufs=5, align_bytes=64)
-                    scales = stage.tile([P, 2 * N], U8, name="w_scales", tag="w_scales", bufs=5, align_bytes=64)
-                interleave(nc, W_ENGINES[unit], grouped[:, half * N * PACK : (half + 1) * N * PACK], raw[:])
-                last = unit == (E - 1) * PASSES - 1
-                if half == 1 or last:
-                    for lo, hi in ((0, 512), (512, 768)) if half == 1 else ((0, 256), (256, 384)):
-                        nc.vector.quantize_mx(
-                            out=codes[:, lo:hi].bitcast(FP8X4),
-                            scales=scales[:, lo:hi],
-                            in_=grouped[:, PACK * lo : PACK * hi],
-                        )
+                engines = W_ENGINES[first_unit + i]
+                width = N // len(engines)
+                for part in range(len(engines)):
+                    lo = part * width
+                    at = PACK * (i * N + lo)
+                    interleave(nc, engines[part], grouped[:, at : at + PACK * width], raw[:, :, lo : lo + width])
                 gather(GATHERS)
-                pending.append((e, a, codes[:, half * N : (half + 1) * N], scales[:, half * N : (half + 1) * N]))
-                if len(gathers) == 0 and (half == 1 or last):
-                    for pe, pa, pcodes, pscales in pending:
-                        for n in range(BLOCKS):
-                            cols = slice(n * P, (n + 1) * P)
-                            multiply(acc[(pe, n)], pe, pa, pcodes[:, cols], pscales[:, cols])
-                        if pa == PASSES - 1:
-                            for n in range(BLOCKS):
-                                activate(acc[(pe, n)], pe, n)
-                    pending.clear()
-                if unit == 1:
-                    nc.sync.dma_start(out=pos1_sb[:], in_=pos1)
-                    nc.sync.dma_start(out=pos2_sb[:], in_=pos2)
-                unit += 1
+                pending.append((e, a, codes[:, i * N : (i + 1) * N], scales[:, i * N : (i + 1) * N]))
+            lo = 0
+            for words in (512, 256) if size == 2 else (256, 128) if len(engines) == 1 else (128, 128, 128):
+                nc.vector.quantize_mx(
+                    out=codes[:, lo : lo + words].bitcast(FP8X4),
+                    scales=scales[:, lo : lo + words],
+                    in_=grouped[:, PACK * lo : PACK * (lo + words)],
+                )
+                lo += words
+            if first_unit == 0:
+                nc.sync.dma_start(out=pos1_sb[:], in_=pos1)
+                nc.sync.dma_start(out=pos2_sb[:], in_=pos2)
+            first_unit += size
+            if len(gathers) > 0:
+                continue
+            for e, a, w_codes, w_scales in pending:
+                for n in range(BLOCKS):
+                    if e > 1 and a == 0:
+                        acc_tile = psum.tile([P, C], F32, name="acc", tag="acc")
+                        acc[(e, n)] = acc_tile[:]
+                    cols = slice(n * P, (n + 1) * P)
+                    multiply(acc[(e, n)], e, a, w_codes[:, cols], w_scales[:, cols])
+                if a == PASSES - 1 and e > 0:
+                    for n in range(BLOCKS):
+                        if e == 1:
+                            activate(acc[(0, n)], 0, n)
+                        activate(acc[(e, n)], e, n)
+            pending.clear()
 
-        e = E - 1
-        gates = {}
+        gates = []
         for n in range(BLOCKS):
-            acc_tile = psum.tile([P, C], F32, name="acc", tag="acc")
-            acc[(e, n)] = acc_tile
-
-        def load_gate(n):
             gate_sb = stage.tile([P, 2, T], F32, name="gate_sb", tag="raw", bufs=RAW)
             nc.sync.dma_start(out=gate_sb[:], in_=gate[:, n * P : (n + 1) * P, :].rearrange("r p t -> p r t"))
-            gates[n] = gate_sb
-
-        def chunk(blocks, passes, engines):
-            width = len(blocks) * P
-            cols = slice(blocks[0] * P, blocks[0] * P + width)
-            raw = stage.tile([P, len(passes), PACK, width], F32, name="t_raw", tag="raw", bufs=RAW)
-            grouped = stage.tile([P, len(passes) * width * PACK], BF16, name="t_grouped", tag="t_grouped", bufs=3, align_bytes=64)
-            codes = stage.tile([P, len(passes) * width], U32, name="t_codes", tag="t_codes", bufs=4, align_bytes=64)
-            scales = stage.tile([P, len(passes) * width], U8, name="t_scales", tag="t_scales", bufs=4, align_bytes=64)
-            for i, a in enumerate(passes):
-                nc.sync.dma_start(out=raw[:, i], in_=w_rows[e, a, :, :, cols])
-            for i in range(len(passes)):
-                interleave(nc, engines[i], grouped[:, i * width * PACK : (i + 1) * width * PACK], raw[:, i])
-            lo = 0
-            total = len(passes) * width
-            for words in (512, 256, 128):
-                if total - lo >= words:
-                    nc.vector.quantize_mx(
-                        out=codes[:, lo : lo + words].bitcast(FP8X4),
-                        scales=scales[:, lo : lo + words],
-                        in_=grouped[:, PACK * lo : PACK * (lo + words)],
-                    )
-                    lo += words
-            for i, a in enumerate(passes):
-                for n in blocks:
-                    part = slice(i * width + (n - blocks[0]) * P, i * width + (n - blocks[0] + 1) * P)
-                    multiply(acc[(e, n)], e, a, codes[:, part], scales[:, part])
-                    if a == PASSES - 1:
-                        activate(acc[(e, n)], e, n)
+            gates.append(gate_sb)
 
         def combine(n):
-            first = stage.tile([P, T], F32, name="first", tag="first", bufs=2)
-            second = stage.tile([P, T], F32, name="second", tag="second", bufs=2)
+            first = stage.tile([P, T], F32, name="first", tag="first", bufs=3)
+            second = stage.tile([P, T], F32, name="second", tag="second", bufs=3)
             nc.vector.tensor_tensor(out=first[:], in0=y[n][:].indirect(pos1_sb[:]), in1=gates[n][:, 0, :], op=MULT)
             nc.vector.tensor_tensor(out=second[:], in0=y[n][:].indirect(pos2_sb[:]), in1=gates[n][:, 1, :], op=MULT)
             result = stage.tile([P, T], F32, name="result", tag="result", bufs=3)
-            nc.vector.tensor_tensor(out=result[:], in0=first[:], in1=second[:], op=ADD)
+            if n == 0:
+                total = psum.tile([P, T], F32, name="total", tag="acc")
+                nc.tensor.matmul(total[:], identity[:], first[:], start=True, stop=False)
+                nc.tensor.matmul(total[:], identity[:], second[:], start=False, stop=True)
+                nc.scalar.copy(out=result[:], in_=total[:])
+            else:
+                nc.vector.tensor_tensor(out=result[:], in0=first[:], in1=second[:], op=ADD)
             nc.sync.dma_start(out=out[n * P : (n + 1) * P, :], in_=result[:])
 
-        everything = (0, 1, 2)
-        chunk(everything, (0,), "V")
-        chunk(everything, (1,), "V")
-        chunk(everything, (2,), "V")
-        chunk(everything, (3,), "S")
-        chunk((0,), (4,), "S")
-        load_gate(0)
-        chunk((1,), (4,), "V")
-        load_gate(1)
-        combine(0)
-        chunk((2,), (4,), "S")
-        load_gate(2)
-        combine(1)
-        combine(2)
+        for n in range(BLOCKS):
+            combine(n)

@@ -18,124 +18,127 @@ ADD = mybir.AluOpType.add
 
 P = 128
 PACK = 4
-K_PASS = P * PACK
-PASSES = K // K_PASS
+PASSES = K // (P * PACK)
 BLOCKS = N // P
 SLOTS = E * C
-CUTS = ((0, 384), (384, 768), (768, 1024))
+LIST_ROWS = 16
 
 FLOPS = 2 * K * N * E * C
 
-RAW = 12
-X_ENGINES = "SSBSH"
-W_ENGINES = ("S", "S", "S", "S", "S", "S", "S", "S", "S", "S", "H", "V", "V", "V", "V", "H", "V", "V", "W", "SBW")
-GROUP_SIZES = (2, 2, 2, 2, 2, 2, 2, 1, 2, 2, 1)
-GATHERS = 4
-SPLITS = {
-    "V": (("V", 1.0),),
-    "S": (("S", 1.0),),
-    "G": (("G", 1.0),),
-    "B": (("S", 2 / 3), ("V", 1 / 3)),
-    "H": (("S", 1 / 2), ("V", 1 / 2)),
-    "W": (("V", 2 / 3), ("S", 1 / 3)),
-    "J": (("S", 2 / 3), ("G", 1 / 3)),
-}
+SLOT_SLICES = ((0, 384), (384, 768), (768, 1024))
+
+PLANES_PER_TILE = 4
+
+FIRST_PASS_CUTS = ((0, T // 2), (T // 2, T))
+
+X_SCALAR_SHARE = (1, 1, 2 / 3, 1, 1 / 2)
+W_SCALAR_SHARE = (1,) * 10 + (1 / 2,) + (0,) * 4 + (1 / 2, 0, 0, 1 / 3)
+LAST_SCALAR_SHARE = (1, 2 / 3, 1 / 3)
+
+GROUPS = ((0, 1), (2, 3), (4, 5), (6, 7), (8, 9), (10, 11), (12, 13), (14,), (15, 16), (17, 18), (19,))
+
+GATHERS_PER_UNIT = 4
+
+RAW_BUFS = 12
+GROUPED_BUFS = 6
+CODE_BUFS = 6
 
 
-def interleave(nc, engine, grouped, raw):
+def interleave(nc, grouped, raw, scalar_share):
     dst = grouped.rearrange("p (c i t) -> p c t i", i=4, t=PACK)
     src = raw.rearrange("p t (c i) -> p c t i", i=4)
-    groups = dst.shape[1]
-    lo = 0
-    for name, share in SPLITS[engine]:
-        hi = groups if name == SPLITS[engine][-1][0] else lo + int(groups * share + 0.5)
-        part = slice(lo, hi)
-        if name == "V":
-            nc.vector.tensor_copy(out=dst[:, part], in_=src[:, part])
-        elif name == "S":
-            nc.scalar.copy(out=dst[:, part], in_=src[:, part])
-        else:
-            for i in range(4):
-                step = (hi - lo) // 4
-                part = slice(lo + i * step, lo + (i + 1) * step)
-                nc.gpsimd.tensor_scalar(out=dst[:, part], in0=src[:, part], scalar1=1.0, scalar2=0.0, op0=MULT, op1=ADD)
-        lo = hi
+    quads = dst.shape[1]
+    cut = int(quads * scalar_share + 0.5)
+    if cut > 0:
+        nc.scalar.copy(out=dst[:, :cut], in_=src[:, :cut])
+    if cut < quads:
+        nc.vector.tensor_copy(out=dst[:, cut:], in_=src[:, cut:])
+
+
+def power_of_two_pieces(width):
+    pieces, lo = [], 0
+    for piece in (512, 256, 128):
+        while width - lo >= piece:
+            pieces.append((lo, lo + piece))
+            lo += piece
+    return pieces
 
 
 def tile_routed_moe_kernel(tc, xT, w, b, gate, offs, pos1, pos2, out):
     nc = tc.nc
     with ExitStack() as ctx:
         keep = ctx.enter_context(tc.tile_pool(name="keep", bufs=1))
-        stage = ctx.enter_context(tc.tile_pool(name="stage", bufs=2))
+        ring = ctx.enter_context(tc.tile_pool(name="ring", bufs=2))
         psum = ctx.enter_context(tc.psum_pool(name="psum", bufs=8))
 
-        offs_sb = keep.tile([P, SLOTS // 16], U16, name="offs_sb")
-        pos1_sb = keep.tile([P, T // 16], U16, name="pos1_sb")
-        pos2_sb = keep.tile([P, T // 16], U16, name="pos2_sb")
+        x_rows = xT.rearrange("(a p j) t -> a p j t", p=P, j=PACK)
+        w_rows = w.rearrange("e (a p j) n -> e a p j n", p=P, j=PACK)
+
+        offs_list = keep.tile([P, SLOTS // LIST_ROWS], U16, name="offs_list")
+        pos1_list = keep.tile([P, T // LIST_ROWS], U16, name="pos1_list")
+        pos2_list = keep.tile([P, T // LIST_ROWS], U16, name="pos2_list")
         bias = keep.tile([P, BLOCKS, E], F32, name="bias")
 
-        planes4 = keep.tile([P, T], U8, name="planes4", align_bytes=64)
-        plane1 = keep.tile([P, T], U8, name="plane1", align_bytes=64)
-        slot_planes4 = keep.tile([P, SLOTS], U8, name="slot_planes4", align_bytes=64)
-        slot_plane1 = keep.tile([P, SLOTS], U8, name="slot_plane1", align_bytes=64)
-        nc.gpsimd.memset(planes4[:], 0)
-        nc.gpsimd.memset(plane1[:], 0)
         identity = keep.tile([P, P], F32, name="identity")
         make_identity(nc, identity[:])
 
-        x_rows = xT.rearrange("(g p j) t -> g p j t", p=P, j=PACK)
-        w_rows = w.rearrange("e (g p j) n -> e g p j n", p=P, j=PACK)
+        token_scales, slot_scales = [], []
+        for i in range(0, PASSES, PLANES_PER_TILE):
+            tokens = keep.tile([P, T], U8, name=f"token_scales{i}", align_bytes=64)
+            slots = keep.tile([P, SLOTS], U8, name=f"slot_scales{i}", align_bytes=64)
+            nc.gpsimd.memset(tokens[:], 0)
+            token_scales.append(tokens)
+            slot_scales.append(slots)
 
         x_raw = []
         for a in range(PASSES):
-            raw = stage.tile([P, PACK, T], F32, name="raw", tag="raw", bufs=RAW)
-            for lo, hi in ((0, 256), (256, 512)) if a == 0 else ((0, 512),):
+            raw = ring.tile([P, PACK, T], F32, name="x_raw", tag="raw", bufs=RAW_BUFS)
+            for lo, hi in FIRST_PASS_CUTS if a == 0 else ((0, T),):
                 nc.sync.dma_start(out=raw[:, :, lo:hi], in_=x_rows[a, :, :, lo:hi])
             x_raw.append(raw)
             if a == 0:
-                nc.sync.dma_start(out=offs_sb[:], in_=offs)
+                nc.sync.dma_start(out=offs_list[:], in_=offs)
             if a == 2:
-                nc.sync.dma_start(out=bias[:], in_=b.rearrange("(c p) e -> p c e", p=P))
+                nc.sync.dma_start(out=bias[:], in_=b.rearrange("(n p) e -> p n e", p=P))
 
-        x_codes = []
+        token_codes = []
         for a in range(PASSES):
-            grouped = stage.tile([P, T * PACK], BF16, name="x_grouped", tag="grouped", bufs=6, align_bytes=64)
-            for lo, hi in ((0, 256), (256, 512)) if a == 0 else ((0, 512),):
-                interleave(nc, X_ENGINES[a], grouped[:, PACK * lo : PACK * hi], x_raw[a][:, :, lo:hi])
-            codes = keep.tile([P, T], U32, name=f"x_codes{a}", align_bytes=64)
-            scales = planes4[4 * a : P, :] if a < 4 else plane1[:]
-            nc.vector.quantize_mx(out=codes[:].bitcast(FP8X4), scales=scales, in_=grouped[:])
-            x_codes.append(codes)
+            grouped = ring.tile([P, T * PACK], BF16, name="x_grouped", tag="grouped", bufs=GROUPED_BUFS, align_bytes=64)
+            for lo, hi in FIRST_PASS_CUTS if a == 0 else ((0, T),):
+                interleave(nc, grouped[:, PACK * lo : PACK * hi], x_raw[a][:, :, lo:hi], X_SCALAR_SHARE[a])
+            codes = keep.tile([P, T], U32, name=f"token_codes{a}", align_bytes=64)
+            plane = PACK * (a % PLANES_PER_TILE)
+            nc.vector.quantize_mx(
+                out=codes[:].bitcast(FP8X4), scales=token_scales[a // PLANES_PER_TILE][plane:P, :], in_=grouped[:]
+            )
+            token_codes.append(codes)
 
-        slot_codes = []
-        gathers = []
+        slot_codes, gathers = [], []
         for a in range(PASSES):
             codes = keep.tile([P, SLOTS], U32, name=f"slot_codes{a}", align_bytes=64)
             slot_codes.append(codes)
-            for lo, hi in CUTS:
-                gathers.append((codes, x_codes[a], lo, hi))
-            if a == 3:
-                for lo, hi in CUTS:
-                    gathers.append((slot_planes4, planes4, lo, hi))
-            if a == 4:
-                for lo, hi in CUTS:
-                    gathers.append((slot_plane1, plane1, lo, hi))
+            moves = [(codes, token_codes[a])]
+            if a % PLANES_PER_TILE == PLANES_PER_TILE - 1 or a == PASSES - 1:
+                moves.append((slot_scales[a // PLANES_PER_TILE], token_scales[a // PLANES_PER_TILE]))
+            for dst, window in moves:
+                for lo, hi in SLOT_SLICES:
+                    gathers.append((dst, window, lo, hi))
 
-        def gather(count):
-            for g in range(min(count, len(gathers))):
-                dst, src, lo, hi = gathers[0]
-                gathers.remove(gathers[0])
-                nc.vector.tensor_copy(out=dst[:, lo:hi], in_=src[:].indirect(offs_sb[:, lo // 16 : hi // 16]))
+        def gather_some():
+            for dst, window, lo, hi in gathers[:GATHERS_PER_UNIT]:
+                offsets = offs_list[:, lo // LIST_ROWS : hi // LIST_ROWS]
+                nc.vector.tensor_copy(out=dst[:, lo:hi], in_=window[:].indirect(offsets))
+            return gathers[GATHERS_PER_UNIT:]
 
-        def multiply(acc_tile, e, a, w_codes, w_scales):
-            cols = slice(e * C, (e + 1) * C)
-            planes = slot_planes4[4 * a : P, cols] if a < 4 else slot_plane1[:, cols]
+        def multiply(sums, e, a, codes, scales):
+            slots = slice(e * C, (e + 1) * C)
+            plane = PACK * (a % PLANES_PER_TILE)
             nc.tensor.matmul_mx(
-                out=acc_tile,
-                lhsT=w_codes.bitcast(FP8X4),
-                lhsT_scale=w_scales,
-                rhs=slot_codes[a][:, cols].bitcast(FP8X4),
-                rhs_scale=planes,
+                out=sums,
+                lhsT=codes.bitcast(FP8X4),
+                lhsT_scale=scales,
+                rhs=slot_codes[a][:, slots].bitcast(FP8X4),
+                rhs_scale=slot_scales[a // PLANES_PER_TILE][plane:P, slots],
                 start=(a == 0),
                 stop=(a == PASSES - 1),
             )
@@ -145,84 +148,81 @@ def tile_routed_moe_kernel(tc, xT, w, b, gate, offs, pos1, pos2, out):
             y_block = keep.tile([P, SLOTS], F32, name=f"y{n}")
             y.append(y_block)
 
-        def activate(acc_tile, e, n):
-            nc.scalar.activation(out=y[n][:, e * C : (e + 1) * C], in_=acc_tile, func=RELU, bias=bias[:, n, e : e + 1])
-            if e >= 1:
-                done = y[n][:, 0 : 2 * C] if e == 1 else y[n][:, e * C : (e + 1) * C]
-                nc.scalar.activation(out=done, in_=done, func=SQUARE)
+        def relu(sums, e, n):
+            nc.scalar.activation(
+                out=y[n][:, e * C : (e + 1) * C], in_=sums, func=RELU, bias=bias[:, n, e : e + 1]
+            )
 
-        acc = {}
+        def square(n, first_expert, last_expert):
+            part = y[n][:, first_expert * C : (last_expert + 1) * C]
+            nc.scalar.activation(out=part, in_=part, func=SQUARE)
+
+        sums = {}
         for n in range(BLOCKS):
-            pair = psum.tile([P, 2 * C], F32, name="acc_pair", tag="acc")
-            acc[(0, n)] = pair[:, 0:C]
-            acc[(1, n)] = pair[:, C : 2 * C]
-        units = [(e, a) for e in range(E) for a in range(PASSES)]
-        pending = []
-        first_unit = 0
-        for size in GROUP_SIZES:
-            grouped = stage.tile([P, size * N * PACK], BF16, name="w_grouped", tag="grouped", bufs=6, align_bytes=64)
-            codes = stage.tile([P, size * N], U32, name="w_codes", tag="w_codes", bufs=6, align_bytes=64)
-            scales = stage.tile([P, size * N], U8, name="w_scales", tag="w_scales", bufs=6, align_bytes=64)
-            for i in range(size):
-                e, a = units[first_unit + i]
-                raw = stage.tile([P, PACK, N], F32, name="w_raw", tag="raw", bufs=RAW)
+            pair = psum.tile([P, 2 * C], F32, name="pair", tag="bank")
+            sums[(0, n)] = pair[:, 0:C]
+            sums[(1, n)] = pair[:, C : 2 * C]
+
+        waiting = []
+        for group in GROUPS:
+            width = len(group) * N
+            last = group == GROUPS[-1]
+            grouped = ring.tile([P, width * PACK], BF16, name="w_grouped", tag="grouped", bufs=GROUPED_BUFS, align_bytes=64)
+            codes = ring.tile([P, width], U32, name="w_codes", tag="w_codes", bufs=CODE_BUFS, align_bytes=64)
+            scales = ring.tile([P, width], U8, name="w_scales", tag="w_scales", bufs=CODE_BUFS, align_bytes=64)
+            for i, unit in enumerate(group):
+                e, a = unit // PASSES, unit % PASSES
+                raw = ring.tile([P, PACK, N], F32, name="w_raw", tag="raw", bufs=RAW_BUFS)
                 nc.sync.dma_start(out=raw[:], in_=w_rows[e, a])
-                engines = W_ENGINES[first_unit + i]
-                width = N // len(engines)
-                for part in range(len(engines)):
-                    lo = part * width
+                shares = LAST_SCALAR_SHARE if last else (W_SCALAR_SHARE[unit],)
+                step = N // len(shares)
+                for part, share in enumerate(shares):
+                    lo = part * step
                     at = PACK * (i * N + lo)
-                    interleave(nc, engines[part], grouped[:, at : at + PACK * width], raw[:, :, lo : lo + width])
-                gather(GATHERS)
-                pending.append((e, a, codes[:, i * N : (i + 1) * N], scales[:, i * N : (i + 1) * N]))
-            lo = 0
-            for words in (512, 256) if size == 2 else (256, 128) if len(engines) == 1 else (128, 128, 128):
+                    interleave(nc, grouped[:, at : at + PACK * step], raw[:, :, lo : lo + step], share)
+                gathers = gather_some()
+                waiting.append((e, a, codes[:, i * N : (i + 1) * N], scales[:, i * N : (i + 1) * N]))
+            pieces = [(n * P, (n + 1) * P) for n in range(BLOCKS)] if last else power_of_two_pieces(width)
+            for lo, hi in pieces:
                 nc.vector.quantize_mx(
-                    out=codes[:, lo : lo + words].bitcast(FP8X4),
-                    scales=scales[:, lo : lo + words],
-                    in_=grouped[:, PACK * lo : PACK * (lo + words)],
+                    out=codes[:, lo:hi].bitcast(FP8X4), scales=scales[:, lo:hi], in_=grouped[:, PACK * lo : PACK * hi]
                 )
-                lo += words
-            if first_unit == 0:
-                nc.sync.dma_start(out=pos1_sb[:], in_=pos1)
-                nc.sync.dma_start(out=pos2_sb[:], in_=pos2)
-            first_unit += size
             if len(gathers) > 0:
                 continue
-            for e, a, w_codes, w_scales in pending:
+            for e, a, unit_codes, unit_scales in waiting:
                 for n in range(BLOCKS):
                     if e > 1 and a == 0:
-                        acc_tile = psum.tile([P, C], F32, name="acc", tag="acc")
-                        acc[(e, n)] = acc_tile[:]
-                    cols = slice(n * P, (n + 1) * P)
-                    multiply(acc[(e, n)], e, a, w_codes[:, cols], w_scales[:, cols])
-                if a == PASSES - 1 and e > 0:
+                        bank = psum.tile([P, C], F32, name="bank", tag="bank")
+                        sums[(e, n)] = bank[:]
+                    features = slice(n * P, (n + 1) * P)
+                    multiply(sums[(e, n)], e, a, unit_codes[:, features], unit_scales[:, features])
+                if e > 0 and a == PASSES - 1:
                     for n in range(BLOCKS):
                         if e == 1:
-                            activate(acc[(0, n)], 0, n)
-                        activate(acc[(e, n)], e, n)
-            pending.clear()
+                            relu(sums[(0, n)], 0, n)
+                        relu(sums[(e, n)], e, n)
+                        square(n, 0 if e == 1 else e, e)
+            waiting.clear()
 
+        nc.sync.dma_start(out=pos1_list[:], in_=pos1)
+        nc.sync.dma_start(out=pos2_list[:], in_=pos2)
         gates = []
         for n in range(BLOCKS):
-            gate_sb = stage.tile([P, 2, T], F32, name="gate_sb", tag="raw", bufs=RAW)
-            nc.sync.dma_start(out=gate_sb[:], in_=gate[:, n * P : (n + 1) * P, :].rearrange("r p t -> p r t"))
-            gates.append(gate_sb)
+            gate_block = ring.tile([P, 2, T], F32, name="gate_block", tag="raw", bufs=RAW_BUFS)
+            nc.sync.dma_start(out=gate_block[:], in_=gate[:, n * P : (n + 1) * P, :].rearrange("r p t -> p r t"))
+            gates.append(gate_block)
 
-        def combine(n):
-            first = stage.tile([P, T], F32, name="first", tag="first", bufs=3)
-            second = stage.tile([P, T], F32, name="second", tag="second", bufs=3)
-            nc.vector.tensor_tensor(out=first[:], in0=y[n][:].indirect(pos1_sb[:]), in1=gates[n][:, 0, :], op=MULT)
-            nc.vector.tensor_tensor(out=second[:], in0=y[n][:].indirect(pos2_sb[:]), in1=gates[n][:, 1, :], op=MULT)
-            result = stage.tile([P, T], F32, name="result", tag="result", bufs=3)
+        for n in range(BLOCKS):
+            first = ring.tile([P, T], F32, name="first", tag="first", bufs=BLOCKS)
+            second = ring.tile([P, T], F32, name="second", tag="second", bufs=BLOCKS)
+            nc.vector.tensor_tensor(out=first[:], in0=y[n][:].indirect(pos1_list[:]), in1=gates[n][:, 0, :], op=MULT)
+            nc.vector.tensor_tensor(out=second[:], in0=y[n][:].indirect(pos2_list[:]), in1=gates[n][:, 1, :], op=MULT)
+            result = ring.tile([P, T], F32, name="result", tag="result", bufs=BLOCKS)
             if n == 0:
-                total = psum.tile([P, T], F32, name="total", tag="acc")
+                total = psum.tile([P, T], F32, name="total", tag="bank")
                 nc.tensor.matmul(total[:], identity[:], first[:], start=True, stop=False)
                 nc.tensor.matmul(total[:], identity[:], second[:], start=False, stop=True)
                 nc.scalar.copy(out=result[:], in_=total[:])
             else:
                 nc.vector.tensor_tensor(out=result[:], in0=first[:], in1=second[:], op=ADD)
             nc.sync.dma_start(out=out[n * P : (n + 1) * P, :], in_=result[:])
-
-        for n in range(BLOCKS):
-            combine(n)

from contextlib import ExitStack

import concourse.mybir as mybir
from concourse.masks import make_identity

K, T, E, C, N = 2560, 512, 4, 256, 384

F32 = mybir.dt.float32
BF16 = mybir.dt.bfloat16
U32 = mybir.dt.uint32
U16 = mybir.dt.uint16
U8 = mybir.dt.uint8
FP8X4 = mybir.dt.float8_e4m3fn_x4
RELU = mybir.ActivationFunctionType.Relu
SQUARE = mybir.ActivationFunctionType.Square
MULT = mybir.AluOpType.mult
ADD = mybir.AluOpType.add

P = 128
PACK = 4
PASSES = K // (P * PACK)
BLOCKS = N // P
SLOTS = E * C
LIST_ROWS = 16

FLOPS = 2 * K * N * E * C

SLOT_SLICES = ((0, 384), (384, 768), (768, 1024))

PLANES_PER_TILE = 4

FIRST_PASS_CUTS = ((0, T // 2), (T // 2, T))

X_SCALAR_SHARE = (1, 1, 2 / 3, 1, 1 / 2)
W_SCALAR_SHARE = (1,) * 10 + (1 / 2,) + (0,) * 4 + (1 / 2, 0, 0, 1 / 3)
LAST_SCALAR_SHARE = (1, 2 / 3, 1 / 3)

GROUPS = ((0, 1), (2, 3), (4, 5), (6, 7), (8, 9), (10, 11), (12, 13), (14,), (15, 16), (17, 18), (19,))

GATHERS_PER_UNIT = 4

RAW_BUFS = 12
GROUPED_BUFS = 6
CODE_BUFS = 6


def interleave(nc, grouped, raw, scalar_share):
    dst = grouped.rearrange("p (c i t) -> p c t i", i=4, t=PACK)
    src = raw.rearrange("p t (c i) -> p c t i", i=4)
    quads = dst.shape[1]
    cut = int(quads * scalar_share + 0.5)
    if cut > 0:
        nc.scalar.copy(out=dst[:, :cut], in_=src[:, :cut])
    if cut < quads:
        nc.vector.tensor_copy(out=dst[:, cut:], in_=src[:, cut:])


def power_of_two_pieces(width):
    pieces, lo = [], 0
    for piece in (512, 256, 128):
        while width - lo >= piece:
            pieces.append((lo, lo + piece))
            lo += piece
    return pieces


def tile_routed_moe_kernel(tc, xT, w, b, gate, offs, pos1, pos2, out):
    nc = tc.nc
    with ExitStack() as ctx:
        keep = ctx.enter_context(tc.tile_pool(name="keep", bufs=1))
        ring = ctx.enter_context(tc.tile_pool(name="ring", bufs=2))
        psum = ctx.enter_context(tc.psum_pool(name="psum", bufs=8))

        x_rows = xT.rearrange("(a p j) t -> a p j t", p=P, j=PACK)
        w_rows = w.rearrange("e (a p j) n -> e a p j n", p=P, j=PACK)

        offs_list = keep.tile([P, SLOTS // LIST_ROWS], U16, name="offs_list")
        pos1_list = keep.tile([P, T // LIST_ROWS], U16, name="pos1_list")
        pos2_list = keep.tile([P, T // LIST_ROWS], U16, name="pos2_list")
        bias = keep.tile([P, BLOCKS, E], F32, name="bias")

        identity = keep.tile([P, P], F32, name="identity")
        make_identity(nc, identity[:])

        token_scales, slot_scales = [], []
        for i in range(0, PASSES, PLANES_PER_TILE):
            tokens = keep.tile([P, T], U8, name=f"token_scales{i}", align_bytes=64)
            slots = keep.tile([P, SLOTS], U8, name=f"slot_scales{i}", align_bytes=64)
            nc.gpsimd.memset(tokens[:], 0)
            token_scales.append(tokens)
            slot_scales.append(slots)

        x_raw = []
        for a in range(PASSES):
            raw = ring.tile([P, PACK, T], F32, name="x_raw", tag="raw", bufs=RAW_BUFS)
            for lo, hi in FIRST_PASS_CUTS if a == 0 else ((0, T),):
                nc.sync.dma_start(out=raw[:, :, lo:hi], in_=x_rows[a, :, :, lo:hi])
            x_raw.append(raw)
            if a == 0:
                nc.sync.dma_start(out=offs_list[:], in_=offs)
            if a == 2:
                nc.sync.dma_start(out=bias[:], in_=b.rearrange("(n p) e -> p n e", p=P))

        token_codes = []
        for a in range(PASSES):
            grouped = ring.tile([P, T * PACK], BF16, name="x_grouped", tag="grouped", bufs=GROUPED_BUFS, align_bytes=64)
            for lo, hi in FIRST_PASS_CUTS if a == 0 else ((0, T),):
                interleave(nc, grouped[:, PACK * lo : PACK * hi], x_raw[a][:, :, lo:hi], X_SCALAR_SHARE[a])
            codes = keep.tile([P, T], U32, name=f"token_codes{a}", align_bytes=64)
            plane = PACK * (a % PLANES_PER_TILE)
            nc.vector.quantize_mx(
                out=codes[:].bitcast(FP8X4), scales=token_scales[a // PLANES_PER_TILE][plane:P, :], in_=grouped[:]
            )
            token_codes.append(codes)

        slot_codes, gathers = [], []
        for a in range(PASSES):
            codes = keep.tile([P, SLOTS], U32, name=f"slot_codes{a}", align_bytes=64)
            slot_codes.append(codes)
            moves = [(codes, token_codes[a])]
            if a % PLANES_PER_TILE == PLANES_PER_TILE - 1 or a == PASSES - 1:
                moves.append((slot_scales[a // PLANES_PER_TILE], token_scales[a // PLANES_PER_TILE]))
            for dst, window in moves:
                for lo, hi in SLOT_SLICES:
                    gathers.append((dst, window, lo, hi))

        def gather_some():
            for dst, window, lo, hi in gathers[:GATHERS_PER_UNIT]:
                offsets = offs_list[:, lo // LIST_ROWS : hi // LIST_ROWS]
                nc.vector.tensor_copy(out=dst[:, lo:hi], in_=window[:].indirect(offsets))
            return gathers[GATHERS_PER_UNIT:]

        def multiply(sums, e, a, codes, scales):
            slots = slice(e * C, (e + 1) * C)
            plane = PACK * (a % PLANES_PER_TILE)
            nc.tensor.matmul_mx(
                out=sums,
                lhsT=codes.bitcast(FP8X4),
                lhsT_scale=scales,
                rhs=slot_codes[a][:, slots].bitcast(FP8X4),
                rhs_scale=slot_scales[a // PLANES_PER_TILE][plane:P, slots],
                start=(a == 0),
                stop=(a == PASSES - 1),
            )

        y = []
        for n in range(BLOCKS):
            y_block = keep.tile([P, SLOTS], F32, name=f"y{n}")
            y.append(y_block)

        def relu(sums, e, n):
            nc.scalar.activation(
                out=y[n][:, e * C : (e + 1) * C], in_=sums, func=RELU, bias=bias[:, n, e : e + 1]
            )

        def square(n, first_expert, last_expert):
            part = y[n][:, first_expert * C : (last_expert + 1) * C]
            nc.scalar.activation(out=part, in_=part, func=SQUARE)

        sums = {}
        for n in range(BLOCKS):
            pair = psum.tile([P, 2 * C], F32, name="pair", tag="bank")
            sums[(0, n)] = pair[:, 0:C]
            sums[(1, n)] = pair[:, C : 2 * C]

        waiting = []
        for group in GROUPS:
            width = len(group) * N
            last = group == GROUPS[-1]
            grouped = ring.tile([P, width * PACK], BF16, name="w_grouped", tag="grouped", bufs=GROUPED_BUFS, align_bytes=64)
            codes = ring.tile([P, width], U32, name="w_codes", tag="w_codes", bufs=CODE_BUFS, align_bytes=64)
            scales = ring.tile([P, width], U8, name="w_scales", tag="w_scales", bufs=CODE_BUFS, align_bytes=64)
            for i, unit in enumerate(group):
                e, a = unit // PASSES, unit % PASSES
                raw = ring.tile([P, PACK, N], F32, name="w_raw", tag="raw", bufs=RAW_BUFS)
                nc.sync.dma_start(out=raw[:], in_=w_rows[e, a])
                shares = LAST_SCALAR_SHARE if last else (W_SCALAR_SHARE[unit],)
                step = N // len(shares)
                for part, share in enumerate(shares):
                    lo = part * step
                    at = PACK * (i * N + lo)
                    interleave(nc, grouped[:, at : at + PACK * step], raw[:, :, lo : lo + step], share)
                gathers = gather_some()
                waiting.append((e, a, codes[:, i * N : (i + 1) * N], scales[:, i * N : (i + 1) * N]))
            pieces = [(n * P, (n + 1) * P) for n in range(BLOCKS)] if last else power_of_two_pieces(width)
            for lo, hi in pieces:
                nc.vector.quantize_mx(
                    out=codes[:, lo:hi].bitcast(FP8X4), scales=scales[:, lo:hi], in_=grouped[:, PACK * lo : PACK * hi]
                )
            if len(gathers) > 0:
                continue
            for e, a, unit_codes, unit_scales in waiting:
                for n in range(BLOCKS):
                    if e > 1 and a == 0:
                        bank = psum.tile([P, C], F32, name="bank", tag="bank")
                        sums[(e, n)] = bank[:]
                    features = slice(n * P, (n + 1) * P)
                    multiply(sums[(e, n)], e, a, unit_codes[:, features], unit_scales[:, features])
                if e > 0 and a == PASSES - 1:
                    for n in range(BLOCKS):
                        if e == 1:
                            relu(sums[(0, n)], 0, n)
                        relu(sums[(e, n)], e, n)
                        square(n, 0 if e == 1 else e, e)
            waiting.clear()

        nc.sync.dma_start(out=pos1_list[:], in_=pos1)
        nc.sync.dma_start(out=pos2_list[:], in_=pos2)
        gates = []
        for n in range(BLOCKS):
            gate_block = ring.tile([P, 2, T], F32, name="gate_block", tag="raw", bufs=RAW_BUFS)
            nc.sync.dma_start(out=gate_block[:], in_=gate[:, n * P : (n + 1) * P, :].rearrange("r p t -> p r t"))
            gates.append(gate_block)

        for n in range(BLOCKS):
            first = ring.tile([P, T], F32, name="first", tag="first", bufs=BLOCKS)
            second = ring.tile([P, T], F32, name="second", tag="second", bufs=BLOCKS)
            nc.vector.tensor_tensor(out=first[:], in0=y[n][:].indirect(pos1_list[:]), in1=gates[n][:, 0, :], op=MULT)
            nc.vector.tensor_tensor(out=second[:], in0=y[n][:].indirect(pos2_list[:]), in1=gates[n][:, 1, :], op=MULT)
            result = ring.tile([P, T], F32, name="result", tag="result", bufs=BLOCKS)
            if n == 0:
                total = psum.tile([P, T], F32, name="total", tag="bank")
                nc.tensor.matmul(total[:], identity[:], first[:], start=True, stop=False)
                nc.tensor.matmul(total[:], identity[:], second[:], start=False, stop=True)
                nc.scalar.copy(out=result[:], in_=total[:])
            else:
                nc.vector.tensor_tensor(out=result[:], in0=first[:], in1=second[:], op=ADD)
            nc.sync.dma_start(out=out[n * P : (n + 1) * P, :], in_=result[:])
